import numpy as np, ml_dtypes
CORES = [3,11,19,27,35,43,51,59]
N = 8
import mx_ref
BF = ml_dtypes.bfloat16
def tile(rs):
    return np.stack(rs, axis=2).reshape(128, -1).astype(BF)
def pick(q, e):
    c = np.concatenate([q[0].reshape(128, -1, 4), np.zeros((128, 1, 4), np.uint8)], axis=1); s = np.concatenate([q[1], np.ones((16, 1), np.uint8)], axis=1)
    return (np.ascontiguousarray(c[:, e].reshape(128, -1)), np.ascontiguousarray(s[:, e]))
def join(*qs):
    return (np.concatenate([q[0] for q in qs], axis=1), np.concatenate([q[1] for q in qs], axis=1))
def put(q, e, v):
    c, s = q[0].reshape(128, -1, 4).copy(), q[1].copy(); c[:, e] = v[0].reshape(128, -1, 4); s[:, e] = v[1]
    return (c.reshape(128, -1), s)
def pk(c, s):
    return (np.ascontiguousarray(c), mx_ref.live(s))
def emit(q):
    return q[0], q[1]
def packed(v, rng):
    q = [mx_ref.quantize(np.ascontiguousarray(v[r])) for r in range(N)]
    return np.stack([a for a, b in q]), np.stack([mx_ref.plane(b, rng) for a, b in q])
def values_of_codes():
    e, c = np.zeros((128, 128, 4), np.float32), np.zeros((128, 2, 4), np.uint8)
    e[np.arange(128), np.arange(128), 0] = 1
    c[:127, :, 0] = np.arange(256).reshape(2, 128).T[:127]
    return mx_ref.matmul(mx_ref.quantize(e.reshape(128, 512).astype(BF)), (c.reshape(128, 8), np.full((16, 2), 127, np.uint8))).T.reshape(-1).astype(np.float64)
CODE_VALUE, SCALE_VALUE = values_of_codes(), 2.0 ** (np.arange(256) - 127.0)
def decode(q):
    return (CODE_VALUE[q[0]].reshape(16, 8, -1, 4) * SCALE_VALUE[q[1]][:, None, :, None] + 0.0).reshape(128, -1).astype(np.float32)
def f(rng, *shape):
    return mx_ref.flush((rng.standard_normal(shape, dtype=np.float32) * np.exp2(rng.integers(-2, 3, shape[:-1] + (1,)))).astype(BF))
def wide(rng, *shape, cols=0):
    v = rng.standard_normal(shape, dtype=np.float32) * np.exp2(rng.integers(-12, 13, shape)).astype(np.float32)
    if cols: v *= np.repeat(np.exp2(rng.integers(-cols, cols + 1, shape[:-2] + (1, shape[-1] // 4))) * (rng.random(shape[:-2] + (1, shape[-1] // 4)) > 0.0625), 4, axis=-1).astype(np.float32)
    return mx_ref.flush(v.astype(BF))
C, H = 384, 128
DIST = [1, 2, 4]
def numbers_of(rng):
    return {"x": np.array(f(rng, N, 128, 4 * C)), "u": np.array(f(rng, N, 128, 512)), "v": np.array(f(rng, N, 128, 512))}
def changes(rng):
    return np.argsort(rng.random((N, 8, 8)), axis=2).astype(np.int32)
def layers(rng, still=[]):
    k = np.exp2(np.argsort(rng.random((N, 128, 1)), axis=1) % 5 - 6.0).astype(np.float32)
    w = np.array(mx_ref.flush((rng.standard_normal((N, 128, 2048), dtype=np.float32) * k).astype(BF))).reshape(N, 8, 16, 4, 8, 16, 4)
    for i in still:
        w[:, :, i] = 0
        w[:, :, :, :, :, i] = 0
    return w
def weights(rng, w):
    c, p = packed(np.ascontiguousarray(w).reshape(N, 128, 2048), rng)
    return {"wc": c, "ws": p}
def edges(rng, x):
    x = x.astype(np.float32).reshape(N, 8, 16, C, 4)
    k = (N, 8, 8, C, 4)
    a = (2 * rng.integers(64, 128, k) + 1) * np.exp2(-7.0 - rng.integers(8, 15, k)) * (rng.integers(0, 2, k) * 2.0 - 1.0)
    a[:, :, 0, :, 0] = 1.96875
    x[:, :, 8:] = a * np.exp2(rng.integers(-2, 3, (N, 8, 1, C, 1)))
    return x
def undecided(u):
    u = u.reshape(N, 128, 128, 4)
    u[:, :, ::16] = 0
    u[:, :, 1:4] = 0
    return u
def setup_inputs(rng):
    return {**numbers_of(rng), "ch": changes(rng), **weights(rng, layers(rng))}
def setup_inputs_ties(rng):
    d = numbers_of(rng)
    x = edges(rng, d["x"])
    k = rng.integers(-1, 2, (N, 8, C)).astype(np.float32)
    o = rng.permutation(N)
    k[o[0]] = 0
    k[o[1]] = rng.integers(0, 2, (8, 1)) * 2.0 - 1.0
    x[:, :, 0] = 0
    x[:, :, 0, :, 0] = k
    u = undecided(d["u"])
    for h in range(0, 128, 16): u[:, h, h, 0] = 1.0
    for b in range(3): u[:, 16 * b, 1 + b, 0] = 1.0
    return {"x": x.reshape(N, 128, 4 * C).astype(BF), "u": u.reshape(N, 128, 512), "v": d["v"], "ch": changes(rng), **weights(rng, layers(rng, [0]))}
def setup_inputs_near(rng):
    d = numbers_of(rng)
    x = d["x"].astype(np.float32).reshape(N, 8, 16, C, 4)
    s = rng.integers(0, 256, (N, 8, C))
    x[:, :, 0] = 0
    x[:, :, 8:] = 0
    x[:, :, 0, :, 0] = rng.integers(0, 2, (N, 8, C)) * 2.0 - 1.0
    for i in range(2): x[:, :, 8 + i] = ((s[:, :, :, None] >> (4 * i + np.arange(4))) & 1) * np.exp2(4.0 * i + np.arange(4) - 23.0)
    x[:, :, 11, :, 0] = 2.0 ** -10
    x[:, :, 12, :, :3] = rng.integers(-1, 2, (N, 8, C, 3)) * 2.0 ** -22
    o = rng.permutation(N) % 4
    x[o == 3, :, 8:] *= np.float32(2.0 ** -7)
    x[o == 3, :, 12:13] *= np.float32(0.5)
    u = undecided(d["u"])
    for r in range(N):
        k = 1.0 if o[r] == 0 else 2.0 ** -30
        for h in range(0, 128, 16):
            u[r, h + 8:h + 10, h] = k
            if o[r] < 2:
                u[r, h, h, 0] = k
                u[r, h + 11, h, 0] = k
        for b in range(3): u[r, 16 * b + 12, 1 + b, b] = k
    return {"x": x.reshape(N, 128, 4 * C).astype(BF), "u": u.reshape(N, 128, 512), "v": d["v"], "ch": changes(rng), **weights(rng, layers(rng, [0, 8, 9, 10, 11, 12, 13, 14, 15]))}
def setup_inputs_calls(rng):
    d = numbers_of(rng)
    x = edges(rng, d["x"])
    x[:, :, 0] = (-(1.0 + 0.125 * rng.permutation(N)) * 2.0 ** -6)[:, None, None, None]
    o = rng.permutation(N) % 2 * 2.0 - 1.0
    u = d["u"].reshape(N, 128, 128, 4)
    u[:, :, 1:4] = 0
    for r in range(N):
        for b in range(3): u[r, 16 * b, 1 + b, b] = float(o[r])
    return {"x": x.reshape(N, 128, 4 * C).astype(BF), "u": u.reshape(N, 128, 512), "v": d["v"], "ch": changes(rng), **weights(rng, layers(rng))}
def setup_inputs_ends(rng):
    d = numbers_of(rng)
    o = np.array([0, 2, 3, 1])[(np.arange(N) + rng.integers(4)) % 4]
    x = 2.0 ** 25 * (1.0 - 0.125 * rng.integers(0, 3, (N, 8, 16, C, 4)))
    x = np.where((o < 2)[:, None, None, None, None], x, 2.0 ** -30 * (1.0 + 0.125 * rng.integers(0, 8, (N, 1, 1, C, 1))))
    x[o == 1] *= rng.integers(0, 2, (1, 1, 1, C, 1)) * 2.0 - 1.0
    u = d["u"].astype(np.float32).reshape(N, 128, 128, 4)
    v = np.zeros((N, 128, 512), np.float32)
    w = np.zeros((N, 128, 4, 128, 4), np.float32)
    i, e = np.arange(128), np.arange(8)
    for r in range(N):
        a = 2.0 ** 30 if o[r] < 2 else 2.0 ** -30
        k = np.full((128, 8, 4), a)
        if o[r] < 2: k *= 1.0 - 0.125 * rng.integers(0, 3, (128, 8, 4))
        t = np.ones(8) if o[r] == 2 else rng.permutation(8) % 2 * 2.0 - 1.0
        u[r][:, ::16] = k * t[None, :, None]
        if o[r] > 1: u[r][:, 16 * rng.permutation(8)[:2]] = 0
        u[r][:, 1:4] = -a if o[r] == 3 else a
        v[r] = a * (rng.integers(0, 2, (128, 512)) * 2.0 - 1.0)
        if o[r] % 2 == 0: w[r] = 0.125
        else:
            for b in range(4): w[r, i, b, i, b] = 64.0 if o[r] == 1 else 2.0 ** -30
    ch = changes(rng)
    ch[o == 0] = (e + 1) % 8
    ch[o == 1] = e
    ch[o == 2] = 7 - e
    return {"x": x.astype(np.float32).reshape(N, 128, 4 * C).astype(BF), "u": u.reshape(N, 128, 512).astype(BF), "v": v.astype(BF), "ch": ch, **weights(rng, w.astype(BF))}
def setup_inputs_spread(rng):
    d = setup_inputs(rng)
    d["x"] = wide(rng, N, 128, 4 * C, cols=6)
    return d
def check_inputs(d):
    b = []
    for k, most in (("x", 2.0 ** 25), ("u", 2.0 ** 30), ("v", 2.0 ** 30)):
        a = np.abs(d[k].astype(np.float32))
        if not (np.isfinite(a).all() and ((a == 0) | (a >= 2.0 ** -30) & (a <= most)).all()): b.append("a value of " + k)
    if not (np.sort(d["ch"], axis=2) == np.arange(8)).all(): b.append("a row of ch")
    none, least, most = [emit(mx_ref.quantize(np.full((128, 16), k, np.float32).astype(BF)))[1][0, 0] for k in (0.0, 2.0 ** -30, 2.0 ** 30)]
    for r in range(N):
        if ((d["wc"][r] == 0x7F) | (d["wc"][r] == 0xFF)).any(): b.append("wc: a code that is no number")
        s = mx_ref.live(d["ws"][r])
        if ((s != none) & ((s < least) | (s > most))).any(): b.append("ws: a scale out of range")
        a = np.abs(decode(pk(d["wc"][r], d["ws"][r])).astype(np.float64)).reshape(128, 512, 4)
        if not (np.sum(a, axis=(0, 2)) <= 64).all(): b.append("sizes in a column of W")
    return b
def reference(x, u, v, ch, wc, ws):
    qu = [mx_ref.quantize(u[r]) for r in range(N)]
    lay = [pk(wc[r], ws[r]) for r in range(N)]
    now = [x[r] for r in range(N)]
    last = [None] * N
    for d in DIST:
        rung = []
        for r in range(N):
            q = mx_ref.quantize(now[r])
            s = mx_ref.matmul(qu[r], q) + np.float32(0.0)
            order = np.argsort(-s[::16], axis=1, kind="stable")
            a = ch[r][4 * (s[1] > 0) + 2 * (s[2] > 0) + (s[3] > 0)]
            row = np.array(a)
            for j in range(1, C): row[j] = row[j - 1][a[j]]
            h = np.ascontiguousarray(row.T)
            c = np.take_along_axis(order, h, axis=0)
            parts = decode(q).astype(BF).reshape(8, 16, C, 4)
            rung.append(np.ascontiguousarray(parts[h, :, c].transpose(0, 2, 1, 3)).reshape(128, 4 * C))
            last[r] = h
        sent = [mx_ref.quantize(np.ascontiguousarray(rung[r][:, :4 * H])) for r in range(N)]
        for r in range(N):
            came = sent[(r - d) % N]
            own = decode(came)
            first = tile([np.maximum(mx_ref.matmul(pick(lay[r], np.arange(128 * b, 128 * b + 128)), came), np.float32(0.0)) * np.float32(0.03125) + own[:, b::4] for b in range(4)])
            now[r] = np.concatenate([first, rung[r][:, 4 * H:]], axis=1)
    y, rw = np.zeros((N, 128, C), np.float32), np.zeros((N, 8, C), np.float32)
    oc, osc = np.zeros((N, 128, 4 * C), np.uint8), np.zeros((N, 16, C), np.uint8)
    for r in range(N):
        q = mx_ref.quantize(now[r])
        y[r] = mx_ref.matmul(mx_ref.quantize(v[r]), q)
        rw[r] = last[r]
        oc[r], osc[r] = emit(q)
    return {"y": y, "rw": rw, "oc": oc, "osc": osc}

from concourse.mybir import dt, AluOpType as A, ActivationFunctionType as AF

C, H = 384, 128
DIST = [1, 2, 4]
PARTS = ((0, H), (H, C))
NS = 24
W = C + NS
BIG, TINY = 2.0 ** 99, 2.0 ** -120
STEP = 2.0 ** -24 * 1.25
L = 12
M = 48 // L
NC = M // 2
LOGM = {8: 3, 4: 2}[M]
VS = 3
FILL = (9, 1, 6, 2, 2)
EARLY = 4

SCRATCH = {"ps": ("psum", [128, 4096], "float32")}


def _sb(name, n, dtype="float32"):
    SCRATCH[name] = ("sbuf", [128, n], dtype)


for _n, _k in (("u", 128), ("v", 128), ("w", 512), ("e", 512), ("c", 128), ("m", 128), ("ub", 128), ("x0", C), ("x1", C),
               ("x2", C), ("x3", C), ("t0", H), ("t1", H), ("t2", H), ("a0", H), ("a1", H), ("a2", H)):
    _sb("q" + _n, _k, "float8_e4m3fn_x4")
    _sb("s" + _n, _k, "uint8")
for _n, _k in (("ut", 512), ("vt", 512), ("xt", 4 * C), ("et", 2048), ("ones", 512), ("ct", 512), ("mov", 512),
               ("hh", 8 * 4 * C), ("cmp", NS * W), ("scb", NS // VS * (W // 2)), ("junk", 4 * W), ("tt", 4 * C),
               ("xn", 512)):
    _sb(_n, _k, "bfloat16")
for _n, _k in (("pI", 8), ("chi", 8), ("qI", 4), ("qJ", 12), ("fI", 24), ("posI", 24)):
    _sb(_n, _k, "int32")
for _n, _k in (("ubl", 8), ("rol", 24), ("pgl", 2), ("fol", 24), ("fnl", 24), ("lc", 24), ("yl", 24),
               ("dl", M), ("ell", 8), ("posl", 24), ("lt", 96)):
    _sb(_n, _k, "uint16")
for _n, _k in (("pf", 16), ("chf", 32), ("cht", 32), ("row", C), ("ma", C), ("nn", C), ("tmp", C), ("ids", C),
               ("idw", 8 * M), ("lb", 24), ("rho", 24), ("f0", 24), ("f1", 24), ("f2", 24), ("f3", 24), ("f5", 24),
               ("jf", 4), ("ql", 4), ("qa", 4), ("qf", 4), ("io24", 24), ("cd8", 128), ("dm", 64),
               ("sb", C), ("d1", C), ("z", W + NS), ("ab", 2 * NS), ("pos", NS), ("p1", NS), ("p2", NS), ("p3", NS),
               ("orep", C), ("ow", 192), ("kb", 12), ("kk", 4), ("ch8", 192), ("chv", 24), ("lf", 24),
               ("w12", 384), ("wr", 384), ("cv", 24), ("ra", 16 * M + 16), ("rb", 16 * M + 16), ("eb0", 64), ("eb", 64),
               ("et4", 128), ("pa", 128), ("yy", 384), ("yr", 384), ("yn", 384), ("rw8", 24), ("oh", 192), ("sel", 192),
               ("pre", 24), ("pd", 24), ("rl", 512), ("ysb", C)):
    _sb(_n, _k)

SEMAPHORES = ["done_t", "done_v", "done_s", "done_g", "left", "arr0", "arr1", "arr2", "d_x", "d_u", "d_v", "d_w", "d_ch",
              "d_z", "d_h0", "d_h1", "d_cv", "d_e", "d_r", "d_o", "d_y", "d_rw"]


def rank_program(g, core, T, topo):
    rank = T.rank_of(core)
    if rank is None:
        return
    n = len(T.cores)
    Q = {"t": g.tensor, "v": g.vector, "s": g.scalar, "g": g, "y": g.sync}
    OWN = {"t": "done_t", "v": "done_v", "s": "done_s", "g": "done_g"}
    total, waited, tok = {}, {}, {}

    def need(q, sem, val):
        if waited.get((q, sem), 0) < val:
            Q[q].wait_ge(T.sem[sem], val)
            waited[(q, sem)] = val

    def op(q, reads, writes, fn, sem=None, inc=1):
        mine = OWN.get(q) if sem is None else None
        want = {}

        def add(s, v):
            want[s] = max(want.get(s, 0), v)
        for t in reads:
            e = tok.get(t)
            if e:
                if e[0]:
                    add(*e[0])
                if t[:4] == "bank":
                    for s, v in e[1].items():
                        if s != mine:
                            add(s, v)
        for t in writes:
            e = tok.get(t)
            if e:
                if e[0]:
                    add(*e[0])
                for s, v in e[1].items():
                    add(s, v)
        for s in sorted(want):
            need(q, s, want[s])
        out = fn()
        name = sem or mine
        for i in (out if isinstance(out, list) else [out]):
            if i is not None:
                i.then_inc(T.sem[name], inc)
            total[name] = total.get(name, 0) + inc
        me = (name, total[name])
        for t in reads:
            tok.setdefault(t, [None, {}])[1][name] = me[1]
        for t in writes:
            tok[t] = [me, {}]

    def dma(sem, reads, writes, fn, q="y"):
        op(q, reads, writes, fn, sem=sem, inc=16)

    V, S, P, Y = g.vector, g.scalar, g.tensor, g.sync

    def ts(out, i, s1, o1, s2=None, o2=None, r=(), w=()):
        op("v", r, w, lambda: V.tensor_scalar(out, i, s1, s2, o1) if o2 is None else V.tensor_scalar(out, i, s1, s2, o1, o2))

    def tt(out, a, b, o, r=(), w=()):
        op("v", r, w, lambda: V.tensor_tensor(out, a, b, o))

    def cp(out, i, r=(), w=()):
        op("v", r, w, lambda: V.tensor_copy(out, i))

    def act(out, i, f=AF.Copy, r=(), w=(), **k):
        op("s", r, w, lambda: S.activation(out, i, f, **k))

    def ga(out, win, off, r, w):
        act(out, win.indirect(off), r=r, w=w)

    def iota(out, pat, base, cm, w):
        op("g", (), (w,), lambda: g.iota(out, pat, base, cm, allow_small_or_imprecise_dtypes=True))

    def fill(out, c, w):
        op("v", (), (w,), lambda: V.memset(out, c))

    def quant(name, c0, c1, src, r, w):
        op("v", r, (w,), lambda: V.quantize_mx(T["q" + name][:, c0:c1], T["s" + name][:, c0:c1], src))

    def mm(bank, a, a0, b, b0, b1, r):
        op("t", r, ("bank%d" % bank,), lambda: P.matmul_mx(
            T.ps[:, 512 * bank:512 * bank + b1 - b0], T["q" + a][:, a0:a0 + 128], T["s" + a][:, a0:a0 + 128],
            T["q" + b][:, b0:b1], T["s" + b][:, b0:b1], True, True))

    def floordiv(out, x, d, r, w):
        k = out.shape[1]
        ts(T.fI[:, 0:k], x, 1.0 / d, A.mult, -(d - 1) / (2.0 * d), A.add, r=r, w=("fI",))
        cp(out, T.fI[:, 0:k], r=("fI",), w=(w,))

    def slot(m):
        return 16 * m + 8 * (1 - m % 2)

    def names(s, parts):
        return tuple("%s%d" % (s, p) for p in parts)

    def ends(parts):
        return PARTS[parts[0]][0], PARTS[parts[-1]][1]

    pf = lambda i: T.pf[:, i:i + 1]
    SHR, AND = A.arith_shift_right, A.bitwise_and

    dma("d_x", (), ("xt",), lambda: Y.dma_start(T.xt[:], T.x[:]))
    dma("d_u", (), ("ut",), lambda: Y.dma_start(T.ut[:], T.u[:]))
    op("g", (), ("pI0",), lambda: g.iota(T.pI[:, 0:1], [[0, 1]], 0, 1))
    iota(T.jf[:, 0:3], [[128, 3]], 0, 1, "jf")
    iota(T.f5[:, 0:8], [[16, 8]], 0, 0, "f5")
    iota(T.cd8[:], [[1, 16], [0, 8]], 0, 0, "cd8")
    iota(T.io24[:], [[1, 24]], 0, 0, "io24")
    iota(T.row[:], [[1, C]], 0, 0, "row")
    iota(T.lb[:], [[0, L], [16, NC]], 0, 0, "lb")
    iota(T.rho[:], [[0, L], [32, NC]], 8, 0, "rho")
    iota(T.idw[:], [[0, M], [1, 8]], 0, 0, "idw")
    fill(T.chi[:], 0, "chi")
    fill(T.ones[:], 1.0, "ones")
    dma("d_ch", (), ("chi",), lambda: [Y.dma_start(T.chi[32 * a:32 * a + 8, :], T.ch[:, :]) for a in range(4)])
    for b in range(4):
        op("g", ("ones",), ("et%d" % b,), lambda b=b: g.affine_select(
            T.et[:, 512 * b:512 * b + 512], T.ones[:], [[-1, 512]], A.is_equal, 0.0, b, 4))
    iota(T.f0[:], [[16, 24]], 0, 0, "f0")
    iota(T.ra[:, 0:16], [[0, 2], [1, 8]], 0, 0, "ra0")
    iota(T.pa[:, 0:16], [[0, 2], [1, 8]], 0, 0, "pa0")
    iota(T.dm[:], [[0, 4], [1, 16]], 0, 0, "dm")
    iota(T.ids[:], [[4, 24], [96, 16]], 0, 0, "ids")
    dma("d_w", (), ("w",), lambda: [Y.dma_start(T.qw[:].bitcast(dt.uint8), T.wc[:]), Y.dma_start(T.sw[:], T.ws[:])])
    dma("d_v", (), ("vt",), lambda: Y.dma_start(T.vt[:], T.v[:]))

    fill(T.ct[:], 0.0, "ct")
    fill(T.mov[:], 0.0, "mov")
    for i, (s, m) in enumerate(((0, 15), (4, 15), (0, 7), (3, 1), (4, 1))):
        ts(T.pI[:, i + 1:i + 2], T.pI[:, 0:1], s, SHR, m, AND, r=("pI0",), w=("pI%d" % (i + 1),))
    floordiv(T.qf[:, 0:3], T.jf[:, 0:3], L, ("jf",), "qf")
    cp(T.pf[:, 0:5], T.pI[:, 1:6], r=tuple("pI%d" % i for i in range(1, 6)), w=("pf",))
    cp(T.qI[:, 0:3], T.qf[:, 0:3], r=("qf",), w=("qI",))
    ts(T.kb[:, 0:3], T.qf[:, 0:3], -float(L), A.mult, r=("qf",), w=("kb_a",))
    ts(T.qJ[:, 0:3], T.qI[:, 0:3], LOGM, SHR, r=("qI",), w=("qJ0",))
    ts(T.qJ[:, 4:7], T.qI[:, 0:3], 1, AND, r=("qI",), w=("qJ1",))
    ts(T.qJ[:, 8:11], T.qI[:, 0:3], 1, SHR, NC - 1, AND, r=("qI",), w=("qJ2",))
    tt(T.kb[:, 3:6], T.kb[:, 0:3], T.jf[:, 0:3], A.add, r=("kb_a", "jf"), w=("kb_b",))
    cp(T.qa[:, 0:3], T.qJ[:, 0:3], r=("qJ0",), w=("qa",))
    cp(T.kb[:, 9:12], T.qJ[:, 4:7], r=("qJ1",), w=("kb_d",))
    cp(T.ql[:, 0:3], T.qJ[:, 8:11], r=("qJ2",), w=("ql",))
    ts(T.qa[:, 0:3], T.qa[:, 0:3], 2.0, A.mult, r=("qa",), w=("qa",))
    ts(T.kb[:, 6:9], T.kb[:, 3:6], float(NC), A.mult, r=("kb_b",), w=("kb_c",))
    tt(T.qa[:, 0:3], T.qa[:, 0:3], T.kb[:, 9:12], A.add, r=("qa", "kb_d"), w=("qa",))
    tt(T.ql[:, 0:3], T.ql[:, 0:3], T.kb[:, 6:9], A.add, r=("ql", "kb_c"), w=("ql",))
    tok["kb0_0"] = [tok["ql"][0], {}]
    for t in range(3):
        ts(T.ct[:, t::4], T.cd8[:], T.qa[:, t:t + 1], A.is_equal, r=("cd8", "qa", "ct"), w=("ct%d" % t,))
    quant("c", 0, 128, T.ct[:], ("ct", "ct0", "ct1", "ct2"), "c")
    cp(T.ubl[:], T.f5[:, 0:8], r=("f5",), w=("ubl",))
    quant("u", 0, 128, T.ut[:], ("ut",), "u")
    quant("x0", 0, C, T.xt[:], ("xt",), "x0a")
    tok["x0b"] = [tok["x0a"][0], {}]
    op("v", ("u", "ubl"), ("ub",), lambda: V.tensor_copy(
        T.qub[:, 0:128].bitcast(dt.uint32), T.qu[:, 0:128].bitcast(dt.uint32).indirect(T.ubl[:, 0:8])))
    op("v", ("u", "ubl"), ("ubs",), lambda: V.tensor_copy(T.sub[:, 0:128], T.su[:, 0:128].indirect(T.ubl[:, 0:8])))

    def constants_b():
        quant("e", 0, 512, T.et[:], tuple("et%d" % b for b in range(4)), "e")
        for a in range(4):
            cp(T.chf[:, 8 * a:8 * a + 8], T.chi[:], r=("chi",), w=("chf%d" % a,))
        ts(T.pf[:, 5:6], pf(0), 24.0, A.mult, r=("pf",), w=("pf5",))
        ts(T.pf[:, 7:8], pf(3), 8.0, A.mult, r=("pf",), w=("pf7",))
        op("v", tuple("chf%d" % a for a in range(4)), ("cht",),
           lambda: V.transpose(T.cht[:], T.chf[:]))
        ts(T.pf[:, 6:7], pf(5), 24.0, A.add, r=("pf5",), w=("pf6",))
        ts(T.lb[:], T.lb[:], pf(7), A.add, r=("lb", "pf7"), w=("lb",))
        ts(T.rho[:], T.rho[:], pf(7), A.add, r=("rho", "pf7"), w=("rho",))

    def constants_r():
        ts(T.f0[:], T.f0[:], pf(0), A.add, r=("f0", "pf"), w=("f0",))
        floordiv(T.f1[:], T.f0[:], 24, ("f0",), "f1")
        ts(T.f2[:], T.f1[:], -24.0, A.mult, r=("f1",), w=("f2",))
        tt(T.f2[:], T.f2[:], T.f0[:], A.add, r=("f2", "f0"), w=("f2",))
        ts(T.f2[:], T.f2[:], 16.0, A.mult, r=("f2",), w=("f2",))
        tt(T.f2[:], T.f2[:], T.f1[:], A.add, r=("f2", "f1"), w=("f2",))
        cp(T.rol[:], T.f2[:], r=("f2",), w=("rol",))

    def constants_z():
        tm = ("tmp0", "tmp1")
        ts(T.ma[:], T.row[:], pf(5), A.is_lt, r=("row", "pf5"), w=("ma",))
        ts(T.tmp[:], T.row[:], pf(6), A.is_lt, r=("row", "pf6"), w=tm)
        tt(T.tmp[:], T.tmp[:], T.ma[:], A.subtract, r=tm + ("ma",), w=tm)
        ts(T.nn[:], T.ma[:], TINY, A.mult, r=("ma",), w=("nn",))
        ts(T.tmp[:], T.tmp[:], -BIG, A.mult, r=tm, w=tm)
        tt(T.nn[:], T.nn[:], T.tmp[:], A.add, r=tm + ("nn",), w=("nn",))

    def constants_late():
        fill(T.dl[:], 0, "dl")
        fill(T.ell[:], 0, "ell")
        fill(T.pgl[:], 0, "pgl")
        ts(T.dm[:], T.dm[:], pf(0), A.is_equal, r=("dm", "pf"), w=("dm",))
        ts(T.pf[:, 10:11], pf(1), 16.0, A.mult, 8.0, A.add, r=("pf",), w=("pfa",))
        ts(T.pf[:, 11:12], pf(4), -8.0, A.mult, pf(10), A.add, r=("pf", "pfa"), w=("pfb",))
        tt(T.pf[:, 12:13], pf(11), pf(2), A.add, r=("pf", "pfb"), w=("pfc",))
        cp(T.pgl[:, 0:1], pf(12), r=("pfc",), w=("pgl",))
        floordiv(T.f1[:], T.f0[:], 48, ("f0",), "f1")
        ts(T.f2[:], T.f1[:], -48.0, A.mult, r=("f1",), w=("f2",))
        tt(T.f0[:], T.f0[:], T.f2[:], A.add, r=("f0", "f2"), w=("f0",))

        def source(w, lst):
            floordiv(T.f2[:], w, L, ("f0", "f3"), "f2")
            ts(T.f5[:], T.f2[:], -float(L), A.mult, r=("f2",), w=("f5",))
            ts(T.f2[:], T.f2[:], 8.0, A.mult, r=("f2",), w=("f2",))
            tt(T.f5[:], T.f5[:], w, A.add, r=("f5", "f0", "f3"), w=("f5",))
            tt(T.f2[:], T.f2[:], T.f1[:], A.add, r=("f2", "f1"), w=("f2",))
            ts(T.f5[:], T.f5[:], 8.0 * M, A.mult, r=("f5",), w=("f5",))
            tt(T.f5[:], T.f5[:], T.f2[:], A.add, r=("f5", "f2"), w=("f5",))
            cp(T[lst][:], T.f5[:], r=("f5",), w=(lst,))
        source(T.f0[:], "fnl")
        floordiv(T.f2[:], T.f0[:], 3, ("f0",), "f2")
        ts(T.f3[:], T.f2[:], -3.0, A.mult, r=("f2",), w=("f3",))
        tt(T.f3[:], T.f3[:], T.f0[:], A.add, r=("f3", "f0"), w=("f3",))
        ts(T.f3[:], T.f3[:], 16.0, A.mult, r=("f3",), w=("f3",))
        tt(T.f3[:], T.f3[:], T.f2[:], A.add, r=("f3", "f2"), w=("f3",))
        source(T.f3[:], "fol")

    def products(xs, parts):
        c0, c1 = ends(parts)
        xr = tuple(xs + "ab"[p] for p in parts)
        for b in range(c0 // 128, c1 // 128):
            mm(5 + b, xs, 128 * b, "u", 0, 128, xr + ("u",))
        mm(4, "ub", 0, xs, c0, c1, xr + ("ub", "ubs"))

    def numbers(xs, parts):
        c0, c1 = ends(parts)
        for b in range(4):
            mm(b, "e", 128 * b, xs, c0, c1, tuple(xs + "ab"[p] for p in parts) + ("e",))

    def calls(parts):
        t0, t1 = ends(parts)[0] // 128, ends(parts)[1] // 128
        for i, k in enumerate((4.0, 2.0, 1.0)):
            ts(T.kb[:, 3 * i + t0:3 * i + t1], T.ps[:, 2561 + 512 * t0 + i:2050 + 512 * t1 + i:512], 0.0, A.is_gt, k, A.mult,
               r=tuple("bank%d" % (5 + t) for t in range(t0, t1)), w=tuple("kb%d_%d" % (p, i) for p in parts))

    def keep_scores(parts):
        c0, c1 = ends(parts)
        cp(T.sb[:, c0:c1], T.ps[:, 2048:2048 + c1 - c0], r=("bank4",), w=names("sb", parts))
        act(T.d1[:, c0:c1], T.sb[:, c0:c1], AF.Abs, r=names("sb", parts), w=names("d1", parts), scale=STEP)

    def lay_z(parts):
        c0, c1 = ends(parts)
        tm = names("tmp", parts)
        tt(T.tmp[:, c0:c1], T.d1[:, c0:c1], T.ma[:, c0:c1], A.mult, r=names("d1", parts) + ("ma",), w=tm)
        tt(T.tmp[:, c0:c1], T.tmp[:, c0:c1], T.sb[:, c0:c1], A.add, r=tm + names("sb", parts), w=tm)
        tt(T.z[:, NS + c0:NS + c1], T.tmp[:, c0:c1], T.nn[:, c0:c1], A.add, r=tm + ("nn",), w=names("zm", parts))

    def keep_numbers(parts):
        c0, c1 = ends(parts)
        for b in range(4):
            act(T.hh[:, 4 * c0 + b:4 * c1:4], T.ps[:, 512 * b:512 * b + c1 - c0], r=("bank%d" % b,),
                w=tuple("h%d_%d" % (b, p) for p in parts))

    def spread(parts, s0, s1):
        c0, c1 = 4 * ends(parts)[0], 4 * ends(parts)[1]

        def f():
            out = []
            for s in range(s0, s1):
                c, k = slice(1536 * s + c0, 1536 * s + c1), 128 - 16 * s
                out.append(Y.dma_start(T.hh[0:k, c], T.hh[16 * s:128, c0:c1]))
                out.append(Y.dma_start(T.hh[k:128, c], T.hh[0:16 * s, c0:c1]))
            return out
        if s1 > s0:
            dma("d_h1" if s0 > 1 else "d_h0", tuple("h%d_%d" % (b, p) for b in range(4) for p in parts),
                tuple("hx%d_%d" % (p, s) for p in parts for s in range(s0, s1)), f)

    for rd in range(3):
        xs, fresh = "x%d" % rd, ((0,) if rd else (0, 1))
        products(xs, fresh)
        if rd:
            numbers(xs, fresh)
        calls(fresh)
        kbs = tuple("kb%d_%d" % (p, i) for p in (0, 1) for i in range(3))
        tt(T.kk[:, 0:3], T.kb[:, 0:3], T.kb[:, 3:6], A.add, r=kbs, w=("kk",))
        tt(T.kk[:, 0:3], T.kk[:, 0:3], T.kb[:, 6:9], A.add, r=kbs + ("kk",), w=("kk",))
        for t in range(3):
            ts(T.mov[:, t:96:4], T.io24[:], T.ql[:, t:t + 1], A.is_equal, T.kk[:, t:t + 1], A.mult,
               r=("io24", "ql", "kk", "mov"), w=("mov%d" % t,))
        quant("m", 0, 128, T.mov[:], ("mov", "mov0", "mov1", "mov2"), "m")
        mm(5, "c", 0, "m", 0, 128, ("c", "m"))
        keep_scores(fresh)
        dma("d_z", ("sb0", "sb1"), ("zl",), lambda: Y.dma_start(T.z[:, 0:NS], T.sb[0:128:16, :]))
        if rd:
            spread((1,), EARLY, 8)
        else:
            constants_b()
            numbers(xs, fresh)
        for k in range(8):
            ts(T.ch8[:, 24 * k:24 * k + 24], T.ps[:, 2560:2584], float(k), A.is_equal, T.cht[:, k:k + 1], A.mult,
               r=("bank5", "cht"), w=("ch8_%d" % k,))
        c8 = tuple("ch8_%d" % k for k in range(8))
        tt(T.ch8[:, 0:96], T.ch8[:, 0:96], T.ch8[:, 96:192], A.add, r=c8, w=c8)
        tt(T.ch8[:, 0:48], T.ch8[:, 0:48], T.ch8[:, 48:96], A.add, r=c8, w=c8)
        tt(T.chv[:], T.ch8[:, 0:24], T.ch8[:, 24:48], A.add, r=c8, w=("chv",))
        tt(T.lf[:], T.chv[:], T.lb[:], A.add, r=("chv", "lb"), w=("lf",))
        cp(T.lc[:], T.lf[:], r=("lf",), w=("lc",))
        if rd == 0:
            constants_r()
            constants_z()
        keep_numbers(fresh)
        lay_z(fresh)
        ts(T.ab[:, 0:NS], T.z[:, 0:NS], STEP, A.mult, r=("zl",), w=("ab0",))
        ts(T.ab[:, NS:2 * NS], T.z[:, 0:NS], -STEP, A.mult, r=("zl",), w=("ab1",))
        tt(T.ab[:, 0:NS], T.ab[:, 0:NS], T.ab[:, NS:2 * NS], A.max, r=("ab0", "ab1"), w=("ab0",))
        tt(T.ab[:, 0:NS], T.ab[:, 0:NS], T.z[:, 0:NS], A.add, r=("ab0", "zl"), w=("ab0",))
        ts(T.z[:, NS + C:NS + W], T.ab[:, 0:NS], TINY, A.add, r=("ab0",), w=("zr",))

        pend, hw = [], W // 2

        def scan():
            j = pend.pop()
            a = hw * (j // VS)
            op("v", ("cmp%d" % j,), ("scb%d" % j,), lambda: V.tensor_tensor_scan(
                T.scb[:, a:a + hw], T.cmp[:, W * j:W * j + hw], T.cmp[:, W * j + hw:W * j + W], 0.0, A.add, A.add))

        def unit(k):
            z, c = ("zl", "zm0", "zm1", "zr"), T.cmp[:, W * k:W * k + W]
            if k % VS:
                ts(c, T.z[:, k:k + W], T.z[:, k:k + 1], A.is_gt, r=z, w=("cmp%d" % k,))
                act(T.junk[:, W * (k % 4):W * (k % 4) + W], c, r=("cmp%d" % k,), w=("pos%d" % k, "junk%d" % (k % 4)),
                    accum_out=T.pos[:, k:k + 1])
            else:
                ts(c, T.z[:, k:k + W], T.z[:, k:k + 1], A.is_gt, 0.5, A.subtract, r=z, w=("cmp%d" % k,))
            if pend:
                scan()
            if k % VS == 0:
                pend.append(k)
        by_s, by_v = [k for k in range(NS) if k % VS], [k for k in range(0, NS, VS)]

        def some(m, a):
            for _ in range(m):
                if a:
                    unit(a.pop(0))

        wb = 8 * M
        for l in range(L):
            win = T.idw[:] if l == 0 else T.w12[:, wb * (l - 1):wb * l]
            ga(T.w12[:, wb * l:wb * l + wb], win, T.lc[:, NC * l:NC * l + NC],
               ("lc", "w%d" % (l - 1) if l else "idw"), ("w%d" % l,))
        ga(T.wr[:], T.w12[:], T.rol[:], tuple("w%d" % l for l in range(L)) + ("rol",), ("wr",))
        dma("d_cv", ("wr",), ("cv",), lambda: Y.dma_start(T.cv[:], T.wr[0:128:16, :]))
        spread(fresh, 1, 8)
        if rd == 0:
            constants_late()
        some(FILL[1], by_v)
        some(FILL[0], by_s)
        cp(T.dl[:, 0:M:2], T.cv[:, 24 - NC:24], r=("cv", "dl"), w=("dl",))

        def chain(buf, m):
            ga(T[buf][:, 16 * m + 16:16 * m + 32], T[buf][:, slot(m):slot(m) + 8], T.dl[:, 2 * (m // 2):2 * (m // 2) + 1],
               ("%s%d" % (buf, m), "dl"), ("%s%d" % (buf, m + 1),))
        for m in range(M):
            chain("ra", m)
        dma("d_e", ("ra%d" % M,), ("eb0",), lambda: Y.dma_start(T.eb0[0:1, :], T.ra[0:128:16, slot(M):slot(M) + 8]))
        tt(T.lf[:], T.cv[:], T.rho[:], A.add, r=("cv", "rho"), w=("lf",))
        cp(T.yl[:], T.lf[:], r=("lf",), w=("yl",))
        some(FILL[3], by_v)
        some(FILL[2], by_s)
        op("g", ("eb0",), ("eb",), lambda: g.partition_broadcast(T.eb[:], T.eb0[0:1, :], 128))
        tt(T.et4[:, 0:64], T.eb[:], T.dm[:], A.mult, r=("eb", "dm"), w=("et4",))
        for a, o, k in ((0, 64, 32), (64, 96, 16), (96, 112, 8), (112, 120, 4)):
            tt(T.et4[:, o:o + k], T.et4[:, a:a + 2 * k:2], T.et4[:, a + 1:a + 2 * k:2], A.add, r=("et4",), w=("et4",))
        cp(T.ell[:, 0:8:2], T.et4[:, 120:124], r=("et4", "ell"), w=("ell",))
        some(FILL[4], by_v)
        for m in range(7):
            ga(T.pa[:, 16 * m + 16:16 * m + 32], T.pa[:, slot(m):slot(m) + 8], T.ell[:, 2 * (m // 2):2 * (m // 2) + 1],
               ("pa%d" % m, "ell"), ("pa%d" % (m + 1),))
        ga(T.rb[:, 0:16], T.pa[:], T.pgl[:, 0:1], tuple("pa%d" % m for m in range(8)) + ("pgl",), ("rb0",))
        for m in range(M - 1):
            chain("rb", m)
        rbs = tuple("rb%d" % m for m in range(M))
        ga(T.yy[:], T.rb[:, 0:16 * M], T.yl[:], rbs + ("yl",), ("yy",))
        ga(T.yr[:], T.yy[:], T.fol[:], ("yy", "fol"), ("yr",))
        dma("d_r", ("yr",), ("rw8",), lambda: [Y.dma_start(T.rw8[:, 3 * h:3 * h + 3], T.yr[16 * h:16 * h + 1, :])
                                               for h in range(8)])
        some(NS, by_v)
        some(NS, by_s)
        while pend:
            scan()
        if rd == 2:
            ga(T.yn[:], T.yy[:], T.fnl[:], ("yy", "fnl"), ("yn",))
        ts(T.pos[:, 0::VS], T.scb[:, hw - 1::hw], float(hw), A.add, r=tuple("scb%d" % k for k in range(0, NS, VS)), w=("posv",))
        pr = tuple("pos%d" % k for k in range(NS) if k % VS) + ("posv",)
        ts(T.posI[:], T.pos[:], 0.0625, A.mult, -0.46875, A.add, r=pr, w=("posI",))
        ts(T.p1[:], T.pos[:], 24.0, A.mult, r=pr, w=("p1",))
        ts(T.p2[:], T.posI[:], -383.0, A.mult, r=("posI",), w=("p2",))
        tt(T.p3[:], T.p1[:], T.p2[:], A.add, r=("p1", "p2"), w=("p3",))
        cp(T.posl[:], T.p3[:], r=("p3",), w=("posl",))
        op("v", ("posl", "ids"), ("orep",), lambda: V.tensor_copy(T.orep[:].indirect(T.posl[:]), T.ids[:]))
        dma("d_o", ("orep",), ("ow",), lambda: [Y.dma_start(T.ow[:, 24 * h:24 * h + 24], T.orep[16 * h:16 * h + 8, :])
                                                for h in range(8)])
        ts(T.pd[:], T.rw8[:], pf(1), A.subtract, r=("rw8", "pf"), w=("pd",))
        for h in range(8):
            ts(T.oh[:, 24 * h:24 * h + 24], T.rw8[:], float(h), A.is_equal, r=("rw8",), w=("oh%d" % h,))
        ts(T.pre[:], T.pd[:], 0.0, A.is_lt, 8.0, A.mult, r=("pd",), w=("pre",))
        tt(T.pre[:], T.pre[:], T.pd[:], A.add, r=("pre", "pd"), w=("pre",))
        ts(T.pre[:], T.pre[:], 1536.0, A.mult, r=("pre",), w=("pre",))
        tt(T.sel[:], T.oh[:], T.ow[:], A.mult, r=tuple("oh%d" % h for h in range(8)) + ("ow",), w=("sel",))
        for k in (96, 48, 24):
            tt(T.sel[:, 0:k], T.sel[:, 0:k], T.sel[:, k:2 * k], A.add, r=("sel",), w=("sel",))
        tt(T.sel[:, 0:24], T.sel[:, 0:24], T.pre[:], A.add, r=("sel", "pre"), w=("sel",))
        for b in (2, 0, 3, 1):
            ts(T.lt[:, 24 * b:24 * b + 24], T.sel[:, 0:24], float(b), A.add, r=("sel",), w=("lt%d" % b,))
        hs = tuple("h%d_%d" % (b, p) for b in range(4) for p in (0, 1)) + tuple(
            "hx%d_%d" % (p, s) for p in (0, 1) for s in range(1, 8))
        for c0, c1, nm in ((0, 8, "ta"), (8, 24, "tb")):
            for b in range(4):
                out, win = T.tt[:, 64 * c0 + b:64 * c1:4], T.hh[:]
                off = T.lt[:, 24 * b + c0:24 * b + c1]
                r, w = hs + ("lt%d" % b,), ("%s%d" % (nm, b),)
                if b < 2:
                    cp(out, win.indirect(off), r=r, w=w)
                else:
                    ga(out, win, off, r, w)
            if nm == "ta":
                tn = "t%d" % rd
                quant(tn, 0, H, T.tt[:, 0:512], tuple("ta%d" % b for b in range(4)), tn)
                dst, src = T.cores[(rank + DIST[rd]) % n], T.cores[(rank - DIST[rd]) % n]
                rid, pid = topo.addr(dst)[0], topo.addr(dst)[1]
                mask, cnt, arr = topo.mask(core, dst), len(topo.engines(core, dst)), "arr%d" % rd

                def send(out, i):
                    def f():
                        g.remote_dma(out_ap=out, in_ap=i, remote_sem=T.sem[arr], local_sem=T.sem.left, pid=pid,
                                     routing_id=rid, dma_engine_mask=mask)
                    op("g", (tn,), (), f, sem="left", inc=cnt)
                send(T["qa%d" % rd][:, 0:H].bitcast(dt.uint8), T["qt%d" % rd][:, 0:H].bitcast(dt.uint8))
                send(T["sa%d" % rd][:, 0:H], T["st%d" % rd][:, 0:H])
                total[arr] = 2 * len(topo.engines(src, core))
                tok["a%d" % rd] = [(arr, total[arr]), {}]
        nx, an = "x%d" % (rd + 1), "a%d" % rd
        quant(nx, H, C, T.tt[:, 512:1536], tuple("tb%d" % b for b in range(4)), nx + "b")
        if rd == 0:
            quant("v", 0, 128, T.vt[:], ("vt",), "v")
        if rd < 2:
            products(nx, (1,))
            numbers(nx, (1,))
            calls((1,))
            keep_scores((1,))
            keep_numbers((1,))
            spread((1,), 1, EARLY)
            lay_z((1,))
        for b in range(4):
            mm(b, "w", 128 * b, an, 0, H, ("w", an))
            mm(4 + b, "e", 128 * b, an, 0, H, ("e", an))
        for b in range(4):
            act(T.rl[:, 128 * b:128 * b + 128], T.ps[:, 512 * b:512 * b + 128], AF.Relu, r=("bank%d" % b,),
                w=("rl%d" % b,), scale=0.03125)
            tt(T.xn[:, b::4], T.rl[:, 128 * b:128 * b + 128], T.ps[:, 2048 + 512 * b:2048 + 512 * b + 128], A.add,
               r=("rl%d" % b, "bank%d" % (4 + b)), w=("xn%d" % b,))
        quant(nx, 0, H, T.xn[:], tuple("xn%d" % b for b in range(4)), nx + "a")
        if rd == 2:
            dma("d_rw", ("yn",), (), lambda: [Y.dma_start(T.rw[:, 48 * h:48 * h + 48], T.yn[16 * h:16 * h + 1, :])
                                              for h in range(8)])
    mm(0, "v", 0, "x3", 0, C, ("v", "x3a", "x3b"))
    dma("d_y", ("x3a", "x3b"), (), lambda: [Y.dma_start(T.oc[:], T.qx3[:, 0:C].bitcast(dt.uint8))]
        + [Y.dma_start(T.osc[4 * k:4 * k + 4, :], T.sx3[32 * k:32 * k + 4, 0:C]) for k in range(4)])
    cp(T.ysb[:], T.ps[:, 0:C], r=("bank0",), w=("ysb",))
    dma("d_y", ("ysb",), (), lambda: Y.dma_start(T.y[:], T.ysb[:]))
    for s in sorted(total):
        need("g", s, total[s])
